import numpy as np
import ml_dtypes


def mxq(x, axis, fmt="e4m3"):
    dtype, down = {"e4m3": (ml_dtypes.float8_e4m3fn, 7), "e5m2": (ml_dtypes.float8_e5m2, 14)}[fmt]
    v = np.moveaxis(np.asarray(x, np.float32).astype(ml_dtypes.bfloat16).astype(np.float64), axis, -1)
    blocks = v.reshape(v.shape[:-1] + (-1, 32))
    amax = np.abs(blocks).max(-1, keepdims=True)
    byte = np.maximum(np.where(amax > 0, np.frexp(amax)[1] - 1 + 127, 0) - down, 1)
    scale = np.exp2(byte - 127.0)
    codes = (blocks / scale).astype(np.float32).astype(dtype).astype(np.float64)
    return np.moveaxis((codes * scale).reshape(v.shape), -1, axis)


WIDE = False


def mx_kscale(k):
    if not WIDE:
        return np.ones(k)
    levels = np.array([10, -10, 5, -5, 0])
    if k % 512:
        return np.exp2(np.random.permutation(np.resize(levels, k // 32))).repeat(32)
    a = np.empty((k // 512, 16))
    for p in range(k // 512):
        a[p, :8] = np.random.permutation(np.resize(levels, 8))
        for g in range(8):
            far = levels[np.abs(levels - a[p, g]) >= 10]
            a[p, g + 8] = far[np.random.randint(len(far))]
    return np.exp2(a.ravel()).repeat(32)


BF16 = ml_dtypes.bfloat16


def bf(x):
    return np.asarray(x, np.float32).astype(BF16)


def f64(x):
    return np.asarray(x).astype(np.float64)

def planes(Y):
    n, m = Y.shape
    b = f64(bf(Y)).reshape(n // 32, 32, m)
    amax = np.abs(b).max(1)
    byte = np.clip(np.where(amax > 0, np.frexp(amax)[1] - 1 + 127 - 7, 1), 1, 254)
    codes = (b * np.exp2(127.0 - byte)[:, None, :]).reshape(n, m).astype(np.float32).astype(ml_dtypes.float8_e4m3fn).view(np.uint8)
    words = codes.reshape(n // 512, 128, 4, m).transpose(0, 1, 3, 2)
    return np.ascontiguousarray(words), np.ascontiguousarray(byte.astype(np.uint8).reshape(n // 512, 16, m))


N, L, F, Q = 1024, 512, 512, 256


def complex_analysis(frames_q, w_real, w_imag):
    return (frames_q @ mxq(f64(w_real), 0, "e4m3"),
            frames_q @ mxq(f64(w_imag), 0, "e4m3"))


def setup_inputs():
    s, t = mx_kscale(L), mx_kscale(F)
    return {
        "x": bf(np.random.standard_normal((N, L)) * s),
        "wr": bf(np.random.standard_normal((L, F)) / np.sqrt(L) / s[:, None]),
        "wi": bf(np.random.standard_normal((L, F)) / np.sqrt(L) / s[:, None]),
        "vr": bf(np.random.standard_normal((L, F)) / np.sqrt(L) / s[:, None]),
        "vi": bf(np.random.standard_normal((L, F)) / np.sqrt(L) / s[:, None]),
        "g": bf((1.0 + 0.1 * np.random.standard_normal(F)) * t),
        "cb": bf(np.random.standard_normal((F, Q)) / np.sqrt(F) / t[:, None]),
    }


def core(x, wr, wi, vr, vi, g, cb):
    xq = mxq(f64(x), 1, "e4m3")
    xr, xi = complex_analysis(xq, wr, wi)
    yr, yi = complex_analysis(xq, vr, vi)
    num = xr * yr + xi * yi
    den = (xr * xr + xi * xi + 0.2) ** 0.7
    tau = f64(g)[None, :] * num / den
    return mxq(tau, 1, "e4m3") @ mxq(f64(cb), 0, "e4m3")


def reference(x, wr, wi, vr, vi, g, cb):
    R_out = core(x, wr, wi, vr, vi, g, cb)
    words, scales = planes(R_out)
    return R_out, words, scales

@@ -1,0 +1,484 @@
+from contextlib import ExitStack
+
+import concourse.mybir as mybir
+from concourse.masks import make_identity
+
+F32 = mybir.dt.float32
+BF16 = mybir.dt.bfloat16
+I32 = mybir.dt.int32
+U32 = mybir.dt.uint32
+U8 = mybir.dt.uint8
+FP8X4 = mybir.dt.float8_e4m3fn_x4
+ADD = mybir.AluOpType.add
+MULT = mybir.AluOpType.mult
+ACT = mybir.ActivationFunctionType
+
+P = 128
+PACK = 4
+N, L, F, Q = 1024, 512, 512, 256
+GROUPS = 2
+TILES = 8
+FLOPS = 2 * N * L * F * 4 + 2 * N * F * Q
+
+CFG = {"sis": (0, 1, 3, 4, 5, 6), "cis": (0, 1, 3, 4, 5), "nia": (3, 4), "npos": 1, "pg": (("i", 7), ("r", 7)), "nacc": 5, "vi_split": 3, "g_ivr": 1, "vr_split": 3, "e_icb": 7, "vfi": (1, 4, 6), "e_qvi": 7, "g_g": 5, "e_qcb": 8, "npre": 5, "e_qx1": 2, "xc1": 0, "crs": (1,), "e_ivr": 1, "vfr": (3, 4, 5, 7), "nr": 3, "e_qvr": 5, "pfirst": 0, "srg": (0, 2, 4, 5, 6), "k_oq": 6, "cb_v": 1, "nlag": 4, "p7": 0, "x1pos": 0, "g_icb": 3, "e_ivi": 4, "g_ivi": 4, "la": 1}
+
+
+def cf(k, d):
+    return CFG.get(k, d)
+COPY_R_ON_SCALAR = cf("crs", (3, 5, 7))
+COPY_I_ON_SCALAR = cf("cis", ())
+SQ_I_ON_SCALAR = cf("sis", (0, 7))
+SQ_R_ON_GPSIMD = cf("srg", ())
+PROD_ON_GPSIMD = cf("pg", (("r", 1), ("i", 1)))
+NACC = cf("nacc", 4)
+N_IN_ACC = cf("nia", (4, 5))
+
+
+def tile_learnedmodifiedgroupdelaycepstrum_x1_kernel(tc, x, wr, wi, vr, vi, g, cb, out_0, out_1, out_2):
+    nc = tc.nc
+    with ExitStack() as ctx:
+        keep = ctx.enter_context(tc.tile_pool(name="keep", bufs=1))
+        flow = ctx.enter_context(tc.tile_pool(name="flow", bufs=4))
+        psum = ctx.enter_context(tc.psum_pool(name="psum", bufs=NACC))
+        psum_tr = ctx.enter_context(tc.psum_pool(name="psum_tr", bufs=8 - NACC))
+        ctx.enter_context(tc.manual_schedule())
+
+        weights = {}
+        for name, src in (("wr", wr), ("wi", wi), ("vr", vr), ("vi", vi)):
+            weights[name] = dict(
+                src=src,
+                raw=keep.tile([P, PACK, F], BF16, name="raw_" + name, align_bytes=64),
+                grp=keep.tile([P, F * PACK], BF16, name="grp_" + name, align_bytes=64),
+                codes=keep.tile([P, F], U32, name="codes_" + name, align_bytes=64),
+                scales=keep.tile([P, F], U8, name="scales_" + name, align_bytes=64),
+            )
+        cb_raw = keep.tile([P, PACK, Q], BF16, name="cb_raw", align_bytes=64)
+        cb_grp = keep.tile([P, Q * PACK], BF16, name="cb_grp", align_bytes=64)
+        cb_codes = keep.tile([P, Q], U32, name="cb_codes", align_bytes=64)
+        cb_scales = keep.tile([P, Q], U8, name="cb_scales", align_bytes=64)
+        g_raw = keep.tile([P, PACK], BF16, name="g_raw")
+        g_col = keep.tile([P, PACK], F32, name="g_col")
+        x_raw = [keep.tile([P, 4, L], BF16, name=f"x_raw{i}", align_bytes=64) for i in range(GROUPS)]
+        x_grp = [keep.tile([P, 4 * P * PACK], BF16, name=f"x_grp{i}", align_bytes=64) for i in range(GROUPS)]
+        x_codes = [keep.tile([P, 4 * P], U32, name=f"x_codes{i}", align_bytes=64) for i in range(GROUPS)]
+        x_scales = [keep.tile([P, 4 * P], U8, name=f"x_scales{i}", align_bytes=64) for i in range(GROUPS)]
+        xs_r = [keep.tile([P, F], F32, name=f"xs_r{i}") for i in range(TILES)]
+        xs_i = [keep.tile([P, F], F32, name=f"xs_i{i}") for i in range(TILES)]
+        pr_r = [keep.tile([P, F], F32, name=f"pr_r{i}") for i in range(TILES)]
+        pr_i = [keep.tile([P, F], F32, name=f"pr_i{i}") for i in range(TILES)]
+        lnp = [keep.tile([P, PACK, 4 * P], F32, name=f"lnp{i}") for i in range(GROUPS)]
+        ex = [keep.tile([P, PACK, 4 * P], F32, name=f"ex{i}") for i in range(GROUPS)]
+        eg = [keep.tile([P, PACK, 4 * P], F32, name=f"eg{i}") for i in range(GROUPS)]
+        tau = [keep.tile([P, P * PACK], BF16, name=f"tau{i}", align_bytes=64) for i in range(TILES)]
+        tau_codes = [keep.tile([P, P], U32, name=f"tau_codes{i}", align_bytes=64) for i in range(TILES)]
+        tau_scales = [keep.tile([P, P], U8, name=f"tau_scales{i}", align_bytes=64) for i in range(TILES)]
+        o_32 = [keep.tile([P, 4, Q], F32, name=f"o_32_{i}", align_bytes=64) for i in range(GROUPS)]
+        o_16 = [keep.tile([P, Q * PACK], BF16, name=f"o_16_{i}", align_bytes=64) for i in range(GROUPS)]
+        o_codes = [keep.tile([P, Q], U32, name=f"o_codes{i}", align_bytes=64) for i in range(GROUPS)]
+        o_scales = keep.tile([P, GROUPS, Q], U8, name="o_scales", align_bytes=64)
+        ident = keep.tile([P, P], F32, name="ident")
+        warm = keep.tile([P, 1], F32, name="warm")
+
+        def load_w(name):
+            w = weights[name]
+            nc.sync.dma_start(out=w["raw"][:], in_=w["src"].rearrange("(p j) c -> p j c", j=PACK))
+
+        def load_x(grp, t0, t1):
+            src = x[512 * grp : 512 * (grp + 1), :].rearrange("(p t) k -> p t k", t=4)
+            nc.sync.dma_start(out=x_raw[grp][:, t0:t1, :], in_=src[:, t0:t1, :])
+
+        def interleave_views(name):
+            w = weights[name]
+            out = w["grp"][:].rearrange("p (t m j) -> p t m j", t=4, j=PACK)
+            in_ = w["raw"][:].rearrange("p j (m t) -> p t m j", t=4)
+            return out, in_
+
+        def il_vector(name, t0, t1):
+            out, in_ = interleave_views(name)
+            nc.vector.tensor_copy(out=out[:, t0:t1], in_=in_[:, t0:t1])
+
+        def il_scalar(name, t0, t1):
+            out, in_ = interleave_views(name)
+            nc.scalar.copy(out=out[:, t0:t1], in_=in_[:, t0:t1])
+
+        def il_gpsimd(name, t0, t1):
+            out, in_ = interleave_views(name)
+            for t in range(t0, t1):
+                nc.gpsimd.tensor_scalar(out=out[:, t], in0=in_[:, t], scalar1=1.0, scalar2=0.0, op0=MULT, op1=ADD)
+
+        def il_cb():
+            out = cb_grp[:].rearrange("p (c j) -> p c j", j=PACK)
+            in_ = cb_raw[:].rearrange("p j c -> p c j")
+            nc.gpsimd.tensor_scalar(out=out, in0=in_, scalar1=1.0, scalar2=0.0, op0=MULT, op1=ADD)
+
+        def quant_cb():
+            nc.vector.quantize_mx(out=cb_codes[:].bitcast(FP8X4), scales=cb_scales[:], in_=cb_grp[:])
+
+        def quant_w(name, t0=0, t1=4):
+            w = weights[name]
+            cols = slice(P * t0, P * t1)
+            nc.vector.quantize_mx(
+                out=w["codes"][:, cols].bitcast(FP8X4),
+                scales=w["scales"][:, cols],
+                in_=w["grp"][:, PACK * P * t0 : PACK * P * t1],
+            )
+
+
+        x_bank = {}
+
+        def x_transpose(grp, s0, s1):
+            words = x_raw[grp][:].rearrange("p t k -> p (t k)").bitcast(F32)
+            for s in range(s0, s1):
+                if s % 2 == 0:
+                    x_bank[(grp, s // 2)] = psum_tr.tile([P, 2, 2, P], F32, name="tr")
+                base = s * (L // 2)
+                for u in range(2):
+                    nc.tensor.transpose(
+                        x_bank[(grp, s // 2)][:, s % 2, u, :], words[:, base + u : base + L // 2 : 2], ident[:]
+                    )
+
+        def x_copy(grp, s0, s1):
+            out = x_grp[grp][:, 512 * s0 : 512 * s1].bitcast(F32).rearrange("p (t r u) -> p t r u", t=s1 - s0, u=2)
+            src = x_bank[(grp, s0 // 2)][:, s0 % 2 : s0 % 2 + s1 - s0].rearrange("p t u r -> p t r u")
+            nc.scalar.copy(out=out, in_=src)
+
+        def x_quant(grp, s0, s1):
+            cols = slice(P * s0, P * s1)
+            nc.vector.quantize_mx(
+                out=x_codes[grp][:, cols].bitcast(FP8X4),
+                scales=x_scales[grp][:, cols],
+                in_=x_grp[grp][:, 512 * s0 : 512 * s1],
+            )
+
+        bank = {}
+
+        def mx1(kind, name, k):
+            acc = psum.tile([P, F], F32, name="bank")
+            cols = slice(P * (k % 4), P * (k % 4 + 1))
+            w = weights[name]
+            nc.tensor.matmul_mx(
+                out=acc[:],
+                lhsT=x_codes[k // 4][:, cols].bitcast(FP8X4),
+                lhsT_scale=x_scales[k // 4][:, cols],
+                rhs=w["codes"][:].bitcast(FP8X4),
+                rhs_scale=w["scales"][:],
+                start=True,
+                stop=True,
+            )
+            bank[(kind, k)] = acc
+
+        sq = {}
+
+        def sq_scalar(kind, k):
+            s = flow.tile([P, F], F32, name="sq_" + kind)
+            nc.scalar.activation(out=s[:], in_=bank[(kind, k)][:], func=ACT.Square)
+            sq[(kind, k)] = s
+
+        def sq_gpsimd(kind, k):
+            s = flow.tile([P, F], F32, name="sq_" + kind)
+            src = xs_r if kind == "r" else xs_i
+            nc.gpsimd.tensor_tensor(out=s[:], in0=src[k][:], in1=src[k][:], op=MULT)
+            sq[(kind, k)] = s
+
+        def copy_x(kind, k, engine):
+            dst = xs_r[k] if kind == "r" else xs_i[k]
+            if engine == "S":
+                nc.scalar.copy(out=dst[:], in_=bank[(kind, k)][:])
+            else:
+                nc.vector.tensor_copy(out=dst[:], in_=bank[(kind, k)][:])
+
+        def sum_transposed(key, k, first, second):
+            if key == "n" and k in N_IN_ACC:
+                tr = psum.tile([P, PACK, P], F32, name="bank")
+            else:
+                tr = psum_tr.tile([P, PACK, P], F32, name="tr")
+            for t in range(PACK):
+                cols = slice(P * t, P * (t + 1))
+                nc.tensor.matmul(out=tr[:, t, :], lhsT=first[:, cols], rhs=ident[:], is_transpose=True, start=True, stop=False)
+                nc.tensor.matmul(out=tr[:, t, :], lhsT=second[:, cols], rhs=ident[:], is_transpose=True, start=False, stop=True)
+            bank[(key, k)] = tr
+
+        def ln(k):
+            s = k % 4
+            nc.scalar.activation(
+                out=lnp[k // 4][:, :, P * s : P * (s + 1)], in_=bank[("p", k)][:], func=ACT.Ln, bias=0.2
+            )
+
+        def exp(grp, t):
+            nc.scalar.activation(out=ex[grp][:, t, :], in_=lnp[grp][:, t, :], func=ACT.Exp, scale=-0.7)
+
+        def gain(grp, t):
+            nc.gpsimd.tensor_scalar(
+                out=eg[grp][:, t, :], in0=ex[grp][:, t, :], scalar1=g_col[:, t : t + 1], scalar2=0.0, op0=MULT, op1=ADD
+            )
+
+        def prod(kind, k):
+            src, dst = (xs_r, pr_r) if kind == "r" else (xs_i, pr_i)
+            nc.vector.tensor_tensor(out=dst[k][:], in0=bank[("y" + kind, k)][:], in1=src[k][:], op=MULT)
+
+        ys = {}
+
+        def y_copy(kind, k):
+            y = flow.tile([P, F], F32, name="ys")
+            nc.scalar.copy(out=y[:], in_=bank[("y" + kind, k)][:])
+            ys[(kind, k)] = y
+
+        def prod_gpsimd(kind, k):
+            src, dst = (xs_r, pr_r) if kind == "r" else (xs_i, pr_i)
+            nc.gpsimd.tensor_tensor(out=dst[k][:], in0=ys[(kind, k)][:], in1=src[k][:], op=MULT)
+
+        def final(k):
+            s = k % 4
+            nc.vector.tensor_tensor(
+                out=tau[k][:].rearrange("p (n t) -> p n t", t=PACK),
+                in0=bank[("n", k)][:].rearrange("p t n -> p n t"),
+                in1=eg[k // 4][:, :, P * s : P * (s + 1)].rearrange("p t n -> p n t"),
+                op=MULT,
+            )
+
+        def tau_quant(k):
+            nc.vector.quantize_mx(out=tau_codes[k][:].bitcast(FP8X4), scales=tau_scales[k][:], in_=tau[k][:])
+
+        out_bank = {}
+
+        def mx2(k):
+            grp, s = k // 4, k % 4
+            for h in range(2):
+                if s == 0:
+                    out_bank[(grp, h)] = psum.tile([P, 4, P], F32, name="bank")
+                cols = slice(P * h, P * (h + 1))
+                nc.tensor.matmul_mx(
+                    out=out_bank[(grp, h)][:, s, :],
+                    lhsT=tau_codes[k][:].bitcast(FP8X4),
+                    lhsT_scale=tau_scales[k][:],
+                    rhs=cb_codes[:, cols].bitcast(FP8X4),
+                    rhs_scale=cb_scales[:, cols],
+                    start=True,
+                    stop=True,
+                )
+
+        def out_32(grp, h, s0=0, s1=4):
+            nc.scalar.copy(out=o_32[grp][:, s0:s1, P * h : P * (h + 1)], in_=out_bank[(grp, h)][:, s0:s1, :])
+
+        def out_16(grp, h, engine):
+            dst = o_16[grp][:, 512 * h : 512 * (h + 1)].rearrange("p (q t) -> p q t", t=4)
+            src = out_bank[(grp, h)][:].rearrange("p t q -> p q t")
+            if engine == "S":
+                nc.scalar.copy(out=dst, in_=src)
+            else:
+                nc.vector.tensor_copy(out=dst, in_=src)
+
+        def out_quant(grp):
+            nc.vector.quantize_mx(out=o_codes[grp][:].bitcast(FP8X4), scales=o_scales[:, grp, :], in_=o_16[grp][:])
+
+        def store_32(grp, s0=0, s1=4):
+            dst = out_0[512 * grp : 512 * (grp + 1), :].rearrange("(p t) m -> p t m", t=4)
+            nc.sync.dma_start(out=dst[:, s0:s1, :], in_=o_32[grp][:, s0:s1, :])
+
+        def store_codes(grp):
+            nc.sync.dma_start(
+                out=out_1[grp].rearrange("p m t -> p (m t)").bitcast(I32), in_=o_codes[grp][:].bitcast(I32)
+            )
+
+        def store_scales():
+            for quad in range(4):
+                nc.sync.dma_start(
+                    out=out_2[:, 4 * quad : 4 * quad + 4, :].bitcast(I32).rearrange("g q m -> q g m"),
+                    in_=o_scales[32 * quad : 32 * quad + 4, :, :].bitcast(I32),
+                )
+
+        load_w("wr")
+        load_x(0, 0, 1)
+        load_x(0, 1, 2)
+        load_x(0, 2, 4)
+        load_w("wi")
+        load_x(1, 0, 4)
+        load_w("vr")
+        load_w("vi")
+        nc.sync.dma_start(out=cb_raw[:], in_=cb.rearrange("(p j) c -> p j c", j=PACK))
+        nc.sync.dma_start(out=g_raw[:], in_=g.rearrange("(p t) -> p t", t=PACK))
+
+        nc.vector.memset(warm[:], 1.0)
+        nc.scalar.activation(out=warm[:], in_=warm[:], func=ACT.Ln)
+        make_identity(nc, ident[:])
+
+        il_scalar("wr", 2, 3)
+        il_vector("wr", 0, 2)
+        il_gpsimd("wr", 3, 4)
+        x_transpose(0, 0, 1)
+        x_copy(0, 0, 1)
+        x_transpose(0, 1, 2)
+        x_copy(0, 1, 2)
+        x_transpose(0, 2, 4)
+        x_copy(0, 2, 4)
+        quant_w("wr", 0, 2)
+        quant_w("wr", 2, 4)
+        x_quant(0, 0, 1)
+        x_quant(0, 1, 2)
+        mx1("r", "wr", 0)
+        mx1("r", "wr", 1)
+        il_vector("wi", 0, 2)
+        il_gpsimd("wi", 2, 4)
+        x_quant(0, 2, 4)
+        quant_w("wi", 0, 2)
+
+        def use_x(kind, k):
+            cs = COPY_R_ON_SCALAR if kind == "r" else COPY_I_ON_SCALAR
+            gq = (kind == "i" and k not in SQ_I_ON_SCALAR) or (kind == "r" and k in SQ_R_ON_GPSIMD)
+            vfirst = k in cf("vf" + kind, ())
+            if vfirst or gq:
+                copy_x(kind, k, "S" if k in cs else "V")
+                if gq:
+                    sq_gpsimd(kind, k)
+                else:
+                    sq_scalar(kind, k)
+            else:
+                sq_scalar(kind, k)
+                copy_x(kind, k, "S" if k in cs else "V")
+
+        use_x("r", 0)
+        quant_w("wi", 2, 4)
+        if cf("nr", 2) > 2:
+            mx1("r", "wr", 2)
+        x_transpose(1, 0, 2)
+        x_transpose(1, 2, 4)
+        use_x("r", 1)
+        mx1("i", "wi", 0)
+        mx1("i", "wi", 1)
+        if cf("xc1", 0) == 0:
+            x_copy(1, 0, 2)
+            x_copy(1, 2, 4)
+        use_x("i", 0)
+        if cf("xc1", 0) == 1:
+            x_copy(1, 0, 2)
+            x_copy(1, 2, 4)
+        use_x("i", 1)
+
+        def v_extra(step):
+            if step == cf("e_qx1", 2):
+                x_quant(1, 0, 4)
+            if step == cf("e_ivr", 2):
+                il_vector("vr", 0, cf("vr_split", 2))
+            if step == cf("e_qvr", 3):
+                quant_w("vr")
+            if step == cf("e_ivi", 4):
+                il_vector("vi", 0, cf("vi_split", 4))
+            if step == cf("e_qvi", 5):
+                quant_w("vi")
+            if step == cf("e_icb", 9) and cf("cb_v", 0):
+                nc.vector.tensor_copy(
+                    out=cb_grp[:].rearrange("p (c j) -> p c j", j=PACK), in_=cb_raw[:].rearrange("p j c -> p c j")
+                )
+            if step == cf("e_qcb", 13):
+                quant_cb()
+
+        def g_extra(step):
+            if step == cf("g_ivr", 1) and cf("vr_split", 2) < 4:
+                il_gpsimd("vr", cf("vr_split", 2), 4)
+            if step == cf("g_ivi", 3) and cf("vi_split", 4) < 4:
+                il_gpsimd("vi", cf("vi_split", 4), 4)
+            if step == cf("g_icb", 9) and not cf("cb_v", 0):
+                il_cb()
+            if step == cf("g_g", 7):
+                nc.gpsimd.tensor_copy(out=g_col[:], in_=g_raw[:])
+
+        g_extra(1)
+        v_extra(1)
+        lag = cf("lag", 2)
+
+        def p_step(k):
+            sum_transposed("p", k, sq[("r", k)], sq[("i", k)])
+            ln(k)
+
+        def y_step(k):
+            mx1("yr", "vr", k)
+            mx1("yi", "vi", k)
+
+        def prods(k):
+            for kind in ("r", "i"):
+                if (kind, k) in PROD_ON_GPSIMD:
+                    y_copy(kind, k)
+                    prod_gpsimd(kind, k)
+                else:
+                    prod(kind, k)
+
+        la = cf("la", 0)
+        done = 2
+        for k in range(2, TILES):
+            while done <= min(k + la, TILES - 1):
+                if not (done == 2 and cf("nr", 2) > 2):
+                    mx1("r", "wr", done)
+                mx1("i", "wi", done)
+                done += 1
+            if cf("pfirst", 0):
+                p_step(k - lag)
+            use_x("r", k)
+            use_x("i", k)
+            v_extra(k)
+            g_extra(k)
+            if not cf("pfirst", 0):
+                p_step(k - lag)
+        v_extra(8)
+        g_extra(8)
+        y_step(0)
+        p_step(6)
+        prods(0)
+        y_step(1)
+        if lag == 2 and cf("p7", 0) == 0:
+            p_step(7)
+        prods(1)
+        if lag == 2 and cf("p7", 0) == 1:
+            p_step(7)
+        v_extra(9)
+        g_extra(9)
+
+        def exps(grp):
+            for t in range(PACK):
+                exp(grp, t)
+                gain(grp, t)
+
+        exps(0)
+        if cf("x1pos", 0) == 0:
+            exps(1)
+        for k in range(2, 8):
+            y_step(k)
+            prods(k)
+            v_extra(8 + k)
+            g_extra(8 + k)
+            if cf("nlag", 3) <= k < 4 + cf("nlag", 3):
+                sum_transposed("n", k - cf("nlag", 3), pr_r[k - cf("nlag", 3)], pr_i[k - cf("nlag", 3)])
+        if cf("x1pos", 0) == 1:
+            exps(1)
+        for k in range(8 - cf("nlag", 3), cf("npre", 6)):
+            sum_transposed("n", k, pr_r[k], pr_i[k])
+        final(0)
+        for k in range(TILES):
+            if k + 1 < TILES:
+                final(k + 1)
+            tau_quant(k)
+            if cf("npos", 0) == 0 and k >= 1 and cf("npre", 6) + k - 1 < 8:
+                sum_transposed("n", cf("npre", 6) + k - 1, pr_r[cf("npre", 6) + k - 1], pr_i[cf("npre", 6) + k - 1])
+            mx2(k)
+            if cf("npos", 0) == 1 and k >= 1 and cf("npre", 6) + k - 1 < 8:
+                sum_transposed("n", cf("npre", 6) + k - 1, pr_r[cf("npre", 6) + k - 1], pr_i[cf("npre", 6) + k - 1])
+            if k == 3:
+                out_16(0, 0, "S")
+                out_16(0, 1, "S")
+                out_32(0, 1)
+                out_32(0, 0)
+            if k == 5:
+                store_32(0)
+                out_32(1, 0, 0, 2)
+                out_32(1, 1, 0, 2)
+                store_32(1, 0, 2)
+            if k == cf("k_oq", 6):
+                out_quant(0)
+                store_codes(0)
+        out_16(1, 1, "V")
+        out_16(1, 0, "S")
+        out_32(1, 1, 2, 4)
+        out_32(1, 0, 2, 4)
+        out_quant(1)
+        store_32(1, 2, 4)
+        store_codes(1)
+        store_scales()

@@ -20,18 +20,16 @@ GROUPS = 2
 TILES = 8
 FLOPS = 2 * N * L * F * 4 + 2 * N * F * Q
 
-CFG = {"sis": (0, 1, 3, 4, 5, 6), "cis": (0, 1, 3, 4, 5), "nia": (3, 4), "npos": 1, "pg": (("i", 7), ("r", 7)), "nacc": 5, "vi_split": 3, "g_ivr": 1, "vr_split": 3, "e_icb": 7, "vfi": (1, 4, 6), "e_qvi": 7, "g_g": 5, "e_qcb": 8, "npre": 5, "e_qx1": 2, "xc1": 0, "crs": (1,), "e_ivr": 1, "vfr": (3, 4, 5, 7), "nr": 3, "e_qvr": 5, "pfirst": 0, "srg": (0, 2, 4, 5, 6), "k_oq": 6, "cb_v": 1, "nlag": 4, "p7": 0, "x1pos": 0, "g_icb": 3, "e_ivi": 4, "g_ivi": 4, "la": 1}
+CFG = {"lag": 3, "e_qvr": 2, "oe0": "V", "nacc": 6, "xe1": "S", "cs": (("i", 0), ("i", 1), ("i", 2), ("i", 7), ("r", 0), ("r", 1), ("r", 2)), "wr_s": 2, "e_ivr": 0, "plv": 0, "nv": (6, 7), "wi_s": 3, "pv": (0, 1, 6), "oq": 1, "vf": (("i", 2), ("r", 2)), "e_ivi": 1, "xe": "S", "oe1": "S", "e_qvi": 3, "xe0": "V", "f0": 8, "e_qx1": 1, "e_icb": 2, "e_qcb": 5}
 
 
 def cf(k, d):
     return CFG.get(k, d)
-COPY_R_ON_SCALAR = cf("crs", (3, 5, 7))
-COPY_I_ON_SCALAR = cf("cis", ())
-SQ_I_ON_SCALAR = cf("sis", (0, 7))
-SQ_R_ON_GPSIMD = cf("srg", ())
-PROD_ON_GPSIMD = cf("pg", (("r", 1), ("i", 1)))
-NACC = cf("nacc", 4)
-N_IN_ACC = cf("nia", (4, 5))
+COPY_ON_SCALAR = cf("cs", (("r", 0), ("i", 0), ("r", 1), ("i", 1), ("r", 2), ("i", 2)))
+COPY_FIRST = cf("vf", ())
+P_ADD_ON_VECTOR = cf("pv", (0, 1))
+NADD_ON_VECTOR = cf("nv", (7,))
+NACC = cf("nacc", 6)
 
 
 def tile_learnedmodifiedgroupdelaycepstrum_x1_kernel(tc, x, wr, wi, vr, vi, g, cb, out_0, out_1, out_2):
@@ -64,14 +62,14 @@ def tile_learnedmodifiedgroupdelaycepstrum_x1_kernel(tc, x, wr, wi, vr, vi, g, c
         x_scales = [keep.tile([P, 4 * P], U8, name=f"x_scales{i}", align_bytes=64) for i in range(GROUPS)]
         xs_r = [keep.tile([P, F], F32, name=f"xs_r{i}") for i in range(TILES)]
         xs_i = [keep.tile([P, F], F32, name=f"xs_i{i}") for i in range(TILES)]
-        pr_r = [keep.tile([P, F], F32, name=f"pr_r{i}") for i in range(TILES)]
-        pr_i = [keep.tile([P, F], F32, name=f"pr_i{i}") for i in range(TILES)]
+        p_sum = {}
+        pr = {}
         lnp = [keep.tile([P, PACK, 4 * P], F32, name=f"lnp{i}") for i in range(GROUPS)]
         ex = [keep.tile([P, PACK, 4 * P], F32, name=f"ex{i}") for i in range(GROUPS)]
-        eg = [keep.tile([P, PACK, 4 * P], F32, name=f"eg{i}") for i in range(GROUPS)]
-        tau = [keep.tile([P, P * PACK], BF16, name=f"tau{i}", align_bytes=64) for i in range(TILES)]
-        tau_codes = [keep.tile([P, P], U32, name=f"tau_codes{i}", align_bytes=64) for i in range(TILES)]
-        tau_scales = [keep.tile([P, P], U8, name=f"tau_scales{i}", align_bytes=64) for i in range(TILES)]
+        num = [keep.tile([P, PACK, 4 * P], F32, name=f"num{i}") for i in range(GROUPS)]
+        tau = [keep.tile([P, 4 * P * PACK], BF16, name=f"tau{i}", align_bytes=64) for i in range(GROUPS)]
+        tau_codes = [keep.tile([P, 4 * P], U32, name=f"tau_codes{i}", align_bytes=64) for i in range(GROUPS)]
+        tau_scales = [keep.tile([P, 4 * P], U8, name=f"tau_scales{i}", align_bytes=64) for i in range(GROUPS)]
         o_32 = [keep.tile([P, 4, Q], F32, name=f"o_32_{i}", align_bytes=64) for i in range(GROUPS)]
         o_16 = [keep.tile([P, Q * PACK], BF16, name=f"o_16_{i}", align_bytes=64) for i in range(GROUPS)]
         o_codes = [keep.tile([P, Q], U32, name=f"o_codes{i}", align_bytes=64) for i in range(GROUPS)]
@@ -101,15 +99,10 @@ def tile_learnedmodifiedgroupdelaycepstrum_x1_kernel(tc, x, wr, wi, vr, vi, g, c
             out, in_ = interleave_views(name)
             nc.scalar.copy(out=out[:, t0:t1], in_=in_[:, t0:t1])
 
-        def il_gpsimd(name, t0, t1):
-            out, in_ = interleave_views(name)
-            for t in range(t0, t1):
-                nc.gpsimd.tensor_scalar(out=out[:, t], in0=in_[:, t], scalar1=1.0, scalar2=0.0, op0=MULT, op1=ADD)
-
         def il_cb():
             out = cb_grp[:].rearrange("p (c j) -> p c j", j=PACK)
             in_ = cb_raw[:].rearrange("p j c -> p c j")
-            nc.gpsimd.tensor_scalar(out=out, in0=in_, scalar1=1.0, scalar2=0.0, op0=MULT, op1=ADD)
+            nc.vector.tensor_copy(out=out, in_=in_)
 
         def quant_cb():
             nc.vector.quantize_mx(out=cb_codes[:].bitcast(FP8X4), scales=cb_scales[:], in_=cb_grp[:])
@@ -137,10 +130,13 @@ def tile_learnedmodifiedgroupdelaycepstrum_x1_kernel(tc, x, wr, wi, vr, vi, g, c
                         x_bank[(grp, s // 2)][:, s % 2, u, :], words[:, base + u : base + L // 2 : 2], ident[:]
                     )
 
-        def x_copy(grp, s0, s1):
+        def x_copy(grp, s0, s1, engine):
             out = x_grp[grp][:, 512 * s0 : 512 * s1].bitcast(F32).rearrange("p (t r u) -> p t r u", t=s1 - s0, u=2)
             src = x_bank[(grp, s0 // 2)][:, s0 % 2 : s0 % 2 + s1 - s0].rearrange("p t u r -> p t r u")
-            nc.scalar.copy(out=out, in_=src)
+            if engine == "S":
+                nc.scalar.copy(out=out, in_=src)
+            else:
+                nc.vector.tensor_copy(out=out, in_=src)
 
         def x_quant(grp, s0, s1):
             cols = slice(P * s0, P * s1)
@@ -153,15 +149,15 @@ def tile_learnedmodifiedgroupdelaycepstrum_x1_kernel(tc, x, wr, wi, vr, vi, g, c
         bank = {}
 
         def mx1(kind, name, k):
-            acc = psum.tile([P, F], F32, name="bank")
+            acc = psum.tile([P, 4 * P], F32, name="bank")
             cols = slice(P * (k % 4), P * (k % 4 + 1))
             w = weights[name]
             nc.tensor.matmul_mx(
                 out=acc[:],
-                lhsT=x_codes[k // 4][:, cols].bitcast(FP8X4),
-                lhsT_scale=x_scales[k // 4][:, cols],
-                rhs=w["codes"][:].bitcast(FP8X4),
-                rhs_scale=w["scales"][:],
+                lhsT=w["codes"][:, cols].bitcast(FP8X4),
+                lhsT_scale=w["scales"][:, cols],
+                rhs=x_codes[k // 4][:].bitcast(FP8X4),
+                rhs_scale=x_scales[k // 4][:],
                 start=True,
                 stop=True,
             )
@@ -174,12 +170,6 @@ def tile_learnedmodifiedgroupdelaycepstrum_x1_kernel(tc, x, wr, wi, vr, vi, g, c
             nc.scalar.activation(out=s[:], in_=bank[(kind, k)][:], func=ACT.Square)
             sq[(kind, k)] = s
 
-        def sq_gpsimd(kind, k):
-            s = flow.tile([P, F], F32, name="sq_" + kind)
-            src = xs_r if kind == "r" else xs_i
-            nc.gpsimd.tensor_tensor(out=s[:], in0=src[k][:], in1=src[k][:], op=MULT)
-            sq[(kind, k)] = s
-
         def copy_x(kind, k, engine):
             dst = xs_r[k] if kind == "r" else xs_i[k]
             if engine == "S":
@@ -187,57 +177,50 @@ def tile_learnedmodifiedgroupdelaycepstrum_x1_kernel(tc, x, wr, wi, vr, vi, g, c
             else:
                 nc.vector.tensor_copy(out=dst[:], in_=bank[(kind, k)][:])
 
-        def sum_transposed(key, k, first, second):
-            if key == "n" and k in N_IN_ACC:
-                tr = psum.tile([P, PACK, P], F32, name="bank")
-            else:
-                tr = psum_tr.tile([P, PACK, P], F32, name="tr")
-            for t in range(PACK):
-                cols = slice(P * t, P * (t + 1))
-                nc.tensor.matmul(out=tr[:, t, :], lhsT=first[:, cols], rhs=ident[:], is_transpose=True, start=True, stop=False)
-                nc.tensor.matmul(out=tr[:, t, :], lhsT=second[:, cols], rhs=ident[:], is_transpose=True, start=False, stop=True)
-            bank[(key, k)] = tr
+        def p_add(k):
+            eng = nc.vector if k in P_ADD_ON_VECTOR else nc.gpsimd
+            p_sum[k] = flow.tile([P, F], F32, name="p_sum")
+            eng.tensor_tensor(out=p_sum[k][:], in0=sq[("r", k)][:], in1=sq[("i", k)][:], op=ADD)
 
         def ln(k):
-            s = k % 4
-            nc.scalar.activation(
-                out=lnp[k // 4][:, :, P * s : P * (s + 1)], in_=bank[("p", k)][:], func=ACT.Ln, bias=0.2
-            )
+            nc.scalar.activation(out=lnp[k // 4][:, k % 4, :], in_=p_sum[k][:], func=ACT.Ln, bias=0.2)
 
-        def exp(grp, t):
-            nc.scalar.activation(out=ex[grp][:, t, :], in_=lnp[grp][:, t, :], func=ACT.Exp, scale=-0.7)
-
-        def gain(grp, t):
-            nc.gpsimd.tensor_scalar(
-                out=eg[grp][:, t, :], in0=ex[grp][:, t, :], scalar1=g_col[:, t : t + 1], scalar2=0.0, op0=MULT, op1=ADD
-            )
+        def exp(grp, n0, n1):
+            nc.scalar.activation(out=ex[grp][:, :, n0:n1], in_=lnp[grp][:, :, n0:n1], func=ACT.Exp, scale=-0.7)
 
         def prod(kind, k):
-            src, dst = (xs_r, pr_r) if kind == "r" else (xs_i, pr_i)
-            nc.vector.tensor_tensor(out=dst[k][:], in0=bank[("y" + kind, k)][:], in1=src[k][:], op=MULT)
+            src = xs_r if kind == "r" else xs_i
+            pr[(kind, k)] = flow.tile([P, F], F32, name="pr_" + kind)
+            t = k % 4
+            nc.vector.scalar_tensor_tensor(
+                out=pr[(kind, k)][:],
+                in0=bank[("y" + kind, k)][:],
+                scalar=g_col[:, t : t + 1],
+                in1=src[k][:],
+                op0=MULT,
+                op1=MULT,
+            )
 
-        ys = {}
+        def n_add(k):
+            eng = nc.vector if k in NADD_ON_VECTOR else nc.gpsimd
+            eng.tensor_tensor(out=num[k // 4][:, k % 4, :], in0=pr[("r", k)][:], in1=pr[("i", k)][:], op=ADD)
 
-        def y_copy(kind, k):
-            y = flow.tile([P, F], F32, name="ys")
-            nc.scalar.copy(out=y[:], in_=bank[("y" + kind, k)][:])
-            ys[(kind, k)] = y
-
-        def prod_gpsimd(kind, k):
-            src, dst = (xs_r, pr_r) if kind == "r" else (xs_i, pr_i)
-            nc.gpsimd.tensor_tensor(out=dst[k][:], in0=ys[(kind, k)][:], in1=src[k][:], op=MULT)
-
-        def final(k):
-            s = k % 4
+        def final(grp, s0, s1):
+            toks = slice(P * s0, P * s1)
             nc.vector.tensor_tensor(
-                out=tau[k][:].rearrange("p (n t) -> p n t", t=PACK),
-                in0=bank[("n", k)][:].rearrange("p t n -> p n t"),
-                in1=eg[k // 4][:, :, P * s : P * (s + 1)].rearrange("p t n -> p n t"),
+                out=tau[grp][:, 512 * s0 : 512 * s1].rearrange("p (c i t) -> p c t i", i=4, t=PACK),
+                in0=num[grp][:, :, toks].rearrange("p t (c i) -> p c t i", i=4),
+                in1=ex[grp][:, :, toks].rearrange("p t (c i) -> p c t i", i=4),
                 op=MULT,
             )
 
-        def tau_quant(k):
-            nc.vector.quantize_mx(out=tau_codes[k][:].bitcast(FP8X4), scales=tau_scales[k][:], in_=tau[k][:])
+        def tau_quant(grp, s0, s1):
+            cols = slice(P * s0, P * s1)
+            nc.vector.quantize_mx(
+                out=tau_codes[grp][:, cols].bitcast(FP8X4),
+                scales=tau_scales[grp][:, cols],
+                in_=tau[grp][:, 512 * s0 : 512 * s1],
+            )
 
         out_bank = {}
 
@@ -245,12 +228,13 @@ def tile_learnedmodifiedgroupdelaycepstrum_x1_kernel(tc, x, wr, wi, vr, vi, g, c
             grp, s = k // 4, k % 4
             for h in range(2):
                 if s == 0:
-                    out_bank[(grp, h)] = psum.tile([P, 4, P], F32, name="bank")
+                    out_bank[(grp, h)] = psum_tr.tile([P, 4, P], F32, name="tr") if grp == 0 else psum.tile([P, 4, P], F32, name="bank")
                 cols = slice(P * h, P * (h + 1))
+                rows = slice(P * s, P * (s + 1))
                 nc.tensor.matmul_mx(
                     out=out_bank[(grp, h)][:, s, :],
-                    lhsT=tau_codes[k][:].bitcast(FP8X4),
-                    lhsT_scale=tau_scales[k][:],
+                    lhsT=tau_codes[grp][:, rows].bitcast(FP8X4),
+                    lhsT_scale=tau_scales[grp][:, rows],
                     rhs=cb_codes[:, cols].bitcast(FP8X4),
                     rhs_scale=cb_scales[:, cols],
                     start=True,
@@ -287,10 +271,9 @@ def tile_learnedmodifiedgroupdelaycepstrum_x1_kernel(tc, x, wr, wi, vr, vi, g, c
                     in_=o_scales[32 * quad : 32 * quad + 4, :, :].bitcast(I32),
                 )
 
-        load_w("wr")
-        load_x(0, 0, 1)
-        load_x(0, 1, 2)
+        load_x(0, 0, 2)
         load_x(0, 2, 4)
+        load_w("wr")
         load_w("wi")
         load_x(1, 0, 4)
         load_w("vr")
@@ -302,178 +285,133 @@ def tile_learnedmodifiedgroupdelaycepstrum_x1_kernel(tc, x, wr, wi, vr, vi, g, c
         nc.scalar.activation(out=warm[:], in_=warm[:], func=ACT.Ln)
         make_identity(nc, ident[:])
 
-        il_scalar("wr", 2, 3)
-        il_vector("wr", 0, 2)
-        il_gpsimd("wr", 3, 4)
-        x_transpose(0, 0, 1)
-        x_copy(0, 0, 1)
-        x_transpose(0, 1, 2)
-        x_copy(0, 1, 2)
+        x_transpose(0, 0, 2)
+        x_copy(0, 0, 2, "S")
         x_transpose(0, 2, 4)
-        x_copy(0, 2, 4)
-        quant_w("wr", 0, 2)
-        quant_w("wr", 2, 4)
-        x_quant(0, 0, 1)
-        x_quant(0, 1, 2)
-        mx1("r", "wr", 0)
-        mx1("r", "wr", 1)
-        il_vector("wi", 0, 2)
-        il_gpsimd("wi", 2, 4)
-        x_quant(0, 2, 4)
-        quant_w("wi", 0, 2)
+        x_copy(0, 2, 4, cf("xe", "V"))
+        nc.gpsimd.tensor_copy(out=g_col[:], in_=g_raw[:])
 
         def use_x(kind, k):
-            cs = COPY_R_ON_SCALAR if kind == "r" else COPY_I_ON_SCALAR
-            gq = (kind == "i" and k not in SQ_I_ON_SCALAR) or (kind == "r" and k in SQ_R_ON_GPSIMD)
-            vfirst = k in cf("vf" + kind, ())
-            if vfirst or gq:
-                copy_x(kind, k, "S" if k in cs else "V")
-                if gq:
-                    sq_gpsimd(kind, k)
-                else:
-                    sq_scalar(kind, k)
+            eng = "S" if (kind, k) in COPY_ON_SCALAR else "V"
+            if (kind, k) in COPY_FIRST:
+                copy_x(kind, k, eng)
+                sq_scalar(kind, k)
             else:
                 sq_scalar(kind, k)
-                copy_x(kind, k, "S" if k in cs else "V")
+                copy_x(kind, k, eng)
 
+        st = cf("wr_s", 3)
+        il_vector("wr", 0, 2)
+        x_quant(0, 0, 2)
+        x_quant(0, 2, 4)
+        if st < 4:
+            il_scalar("wr", st, 4)
+        if st > 2:
+            il_vector("wr", 2, st)
+        quant_w("wr", 0, 2)
+        mx1("r", "wr", 0)
+        mx1("r", "wr", 1)
+        quant_w("wr", 2, 4)
+        il_vector("wi", 0, cf("wi_s", 4))
+        if cf("wi_s", 4) < 4:
+            il_scalar("wi", cf("wi_s", 4), 4)
         use_x("r", 0)
+        quant_w("wi", 0, 2)
         quant_w("wi", 2, 4)
-        if cf("nr", 2) > 2:
-            mx1("r", "wr", 2)
+        use_x("r", 1)
         x_transpose(1, 0, 2)
         x_transpose(1, 2, 4)
-        use_x("r", 1)
         mx1("i", "wi", 0)
         mx1("i", "wi", 1)
-        if cf("xc1", 0) == 0:
-            x_copy(1, 0, 2)
-            x_copy(1, 2, 4)
-        use_x("i", 0)
-        if cf("xc1", 0) == 1:
-            x_copy(1, 0, 2)
-            x_copy(1, 2, 4)
-        use_x("i", 1)
+        x_copy(1, 0, 2, cf("xe0", "S"))
+        x_copy(1, 2, 4, cf("xe1", "S"))
 
-        def v_extra(step):
-            if step == cf("e_qx1", 2):
+        def early(step):
+            if step == cf("e_qx1", 1):
                 x_quant(1, 0, 4)
-            if step == cf("e_ivr", 2):
-                il_vector("vr", 0, cf("vr_split", 2))
-            if step == cf("e_qvr", 3):
+            if step == cf("e_ivr", 1):
+                il_vector("vr", 0, 4)
+            if step == cf("e_qvr", 1):
                 quant_w("vr")
-            if step == cf("e_ivi", 4):
-                il_vector("vi", 0, cf("vi_split", 4))
-            if step == cf("e_qvi", 5):
+            if step == cf("e_ivi", 1):
+                il_vector("vi", 0, 4)
+            if step == cf("e_qvi", 1):
                 quant_w("vi")
-            if step == cf("e_icb", 9) and cf("cb_v", 0):
-                nc.vector.tensor_copy(
-                    out=cb_grp[:].rearrange("p (c j) -> p c j", j=PACK), in_=cb_raw[:].rearrange("p j c -> p c j")
-                )
-            if step == cf("e_qcb", 13):
+            if step == cf("e_icb", 1):
+                il_cb()
+            if step == cf("e_qcb", 1):
                 quant_cb()
 
-        def g_extra(step):
-            if step == cf("g_ivr", 1) and cf("vr_split", 2) < 4:
-                il_gpsimd("vr", cf("vr_split", 2), 4)
-            if step == cf("g_ivi", 3) and cf("vi_split", 4) < 4:
-                il_gpsimd("vi", cf("vi_split", 4), 4)
-            if step == cf("g_icb", 9) and not cf("cb_v", 0):
-                il_cb()
-            if step == cf("g_g", 7):
-                nc.gpsimd.tensor_copy(out=g_col[:], in_=g_raw[:])
+        def padds(step):
+            for k in range(TILES):
+                if step == k + (cf("plv", 1) if k in P_ADD_ON_VECTOR else 0):
+                    p_add(k)
+                if step == k + cf("lag", 2):
+                    ln(k)
 
-        g_extra(1)
-        v_extra(1)
-        lag = cf("lag", 2)
-
-        def p_step(k):
-            sum_transposed("p", k, sq[("r", k)], sq[("i", k)])
-            ln(k)
-
-        def y_step(k):
-            mx1("yr", "vr", k)
-            mx1("yi", "vi", k)
-
-        def prods(k):
-            for kind in ("r", "i"):
-                if (kind, k) in PROD_ON_GPSIMD:
-                    y_copy(kind, k)
-                    prod_gpsimd(kind, k)
-                else:
-                    prod(kind, k)
-
-        la = cf("la", 0)
-        done = 2
+        early(0)
+        use_x("i", 0)
+        padds(0)
+        use_x("i", 1)
+        early(1)
+        padds(1)
         for k in range(2, TILES):
-            while done <= min(k + la, TILES - 1):
-                if not (done == 2 and cf("nr", 2) > 2):
-                    mx1("r", "wr", done)
-                mx1("i", "wi", done)
-                done += 1
-            if cf("pfirst", 0):
-                p_step(k - lag)
+            mx1("r", "wr", k)
+            mx1("i", "wi", k)
             use_x("r", k)
             use_x("i", k)
-            v_extra(k)
-            g_extra(k)
-            if not cf("pfirst", 0):
-                p_step(k - lag)
-        v_extra(8)
-        g_extra(8)
-        y_step(0)
-        p_step(6)
-        prods(0)
-        y_step(1)
-        if lag == 2 and cf("p7", 0) == 0:
-            p_step(7)
-        prods(1)
-        if lag == 2 and cf("p7", 0) == 1:
-            p_step(7)
-        v_extra(9)
-        g_extra(9)
-
-        def exps(grp):
-            for t in range(PACK):
-                exp(grp, t)
-                gain(grp, t)
-
-        exps(0)
-        if cf("x1pos", 0) == 0:
-            exps(1)
-        for k in range(2, 8):
-            y_step(k)
-            prods(k)
-            v_extra(8 + k)
-            g_extra(8 + k)
-            if cf("nlag", 3) <= k < 4 + cf("nlag", 3):
-                sum_transposed("n", k - cf("nlag", 3), pr_r[k - cf("nlag", 3)], pr_i[k - cf("nlag", 3)])
-        if cf("x1pos", 0) == 1:
-            exps(1)
-        for k in range(8 - cf("nlag", 3), cf("npre", 6)):
-            sum_transposed("n", k, pr_r[k], pr_i[k])
-        final(0)
+            early(k)
+            padds(k)
         for k in range(TILES):
-            if k + 1 < TILES:
-                final(k + 1)
-            tau_quant(k)
-            if cf("npos", 0) == 0 and k >= 1 and cf("npre", 6) + k - 1 < 8:
-                sum_transposed("n", cf("npre", 6) + k - 1, pr_r[cf("npre", 6) + k - 1], pr_i[cf("npre", 6) + k - 1])
+            mx1("yr", "vr", k)
+            mx1("yi", "vi", k)
+            prod("r", k)
+            prod("i", k)
+            early(8 + k)
+            padds(8 + k)
+            if k == cf("lag", 2):
+                exp(0, 0, 256)
+                exp(0, 256, 512)
+                exp(1, 0, 256)
+                exp(1, 256, 512)
+            if k >= 1:
+                n_add(k - 1)
+            if cf("f0", 8) == k:
+                final(0, 0, 2)
+            if cf("f0", 8) + 1 == k:
+                final(0, 2, 4)
+        n_add(7)
+        if cf("f0", 8) > 7:
+            final(0, 0, 2)
+        if cf("f0", 8) > 6:
+            final(0, 2, 4)
+        tau_quant(0, 0, 2)
+        final(1, 0, 2)
+        tau_quant(0, 2, 4)
+        for k in range(4):
             mx2(k)
-            if cf("npos", 0) == 1 and k >= 1 and cf("npre", 6) + k - 1 < 8:
-                sum_transposed("n", cf("npre", 6) + k - 1, pr_r[cf("npre", 6) + k - 1], pr_i[cf("npre", 6) + k - 1])
-            if k == 3:
-                out_16(0, 0, "S")
-                out_16(0, 1, "S")
-                out_32(0, 1)
-                out_32(0, 0)
-            if k == 5:
-                store_32(0)
-                out_32(1, 0, 0, 2)
-                out_32(1, 1, 0, 2)
-                store_32(1, 0, 2)
-            if k == cf("k_oq", 6):
-                out_quant(0)
-                store_codes(0)
+        out_16(0, 0, cf("oe0", "S"))
+        out_16(0, 1, cf("oe1", "S"))
+        out_32(0, 1)
+        out_32(0, 0)
+        store_32(0)
+        final(1, 2, 3)
+        tau_quant(1, 0, 2)
+        mx2(4)
+        mx2(5)
+        out_32(1, 0, 0, 2)
+        out_32(1, 1, 0, 2)
+        store_32(1, 0, 2)
+        final(1, 3, 4)
+        if cf("oq", 1) == 0:
+            out_quant(0)
+        tau_quant(1, 2, 3)
+        mx2(6)
+        tau_quant(1, 3, 4)
+        mx2(7)
+        if cf("oq", 1) == 1:
+            out_quant(0)
+        store_codes(0)
         out_16(1, 1, "V")
         out_16(1, 0, "S")
         out_32(1, 1, 2, 4)

@@ -20,7 +20,7 @@ GROUPS = 2
 TILES = 8
 FLOPS = 2 * N * L * F * 4 + 2 * N * F * Q
 
-CFG = {"lag": 3, "e_qvr": 2, "oe0": "V", "nacc": 6, "xe1": "S", "cs": (("i", 0), ("i", 1), ("i", 2), ("i", 7), ("r", 0), ("r", 1), ("r", 2)), "wr_s": 2, "e_ivr": 0, "plv": 0, "nv": (6, 7), "wi_s": 3, "pv": (0, 1, 6), "oq": 1, "vf": (("i", 2), ("r", 2)), "e_ivi": 1, "xe": "S", "oe1": "S", "e_qvi": 3, "xe0": "V", "f0": 8, "e_qx1": 1, "e_icb": 2, "e_qcb": 5}
+CFG = {"xe0": "S", "e_qvr": 2, "nv": (6, 7), "o5": 0, "e_ivr": 0, "cs": (("i", 0), ("i", 1), ("i", 2), ("i", 3), ("i", 4), ("i", 6), ("i", 7), ("r", 0), ("r", 1), ("r", 5), ("r", 7)), "tq": 2, "pv": (0, 2, 3, 6), "vr_g": 0, "o3": 2, "g_g": 2, "e_ivi": 1, "f0": 8, "vf": (("i", 0), ("i", 3), ("i", 6), ("r", 1), ("r", 5)), "xe1": "S", "nacc": 6, "g_ivr": 1, "e32": 1, "fb": 4, "e_qvi": 3, "e_qcb": 6, "e_icb": 4, "o2": 0, "plv": 0, "tl": 3, "lag": 3, "vi_g": 0, "g_ivi": 5, "nl": 0, "o4": 0, "e_qx1": 2, "nlag": 0, "yin": 1, "dy": 4, "oo": 1, "o6": 0}
 
 
 def cf(k, d):
@@ -36,7 +36,7 @@ def tile_learnedmodifiedgroupdelaycepstrum_x1_kernel(tc, x, wr, wi, vr, vi, g, c
     nc = tc.nc
     with ExitStack() as ctx:
         keep = ctx.enter_context(tc.tile_pool(name="keep", bufs=1))
-        flow = ctx.enter_context(tc.tile_pool(name="flow", bufs=4))
+        flow = ctx.enter_context(tc.tile_pool(name="flow", bufs=cf("fb", 4)))
         psum = ctx.enter_context(tc.psum_pool(name="psum", bufs=NACC))
         psum_tr = ctx.enter_context(tc.psum_pool(name="psum_tr", bufs=8 - NACC))
         ctx.enter_context(tc.manual_schedule())
@@ -87,21 +87,25 @@ def tile_learnedmodifiedgroupdelaycepstrum_x1_kernel(tc, x, wr, wi, vr, vi, g, c
 
         def interleave_views(name):
             w = weights[name]
-            out = w["grp"][:].rearrange("p (t m j) -> p t m j", t=4, j=PACK)
-            in_ = w["raw"][:].rearrange("p j (m t) -> p t m j", t=4)
+            out = w["grp"][:].rearrange("p (t m j) -> p m j t", t=4, j=PACK)
+            in_ = w["raw"][:].rearrange("p j (m t) -> p m j t", t=4)
             return out, in_
 
         def il_vector(name, t0, t1):
             out, in_ = interleave_views(name)
-            nc.vector.tensor_copy(out=out[:, t0:t1], in_=in_[:, t0:t1])
+            nc.vector.tensor_copy(out=out[:, :, :, t0:t1], in_=in_[:, :, :, t0:t1])
 
         def il_scalar(name, t0, t1):
             out, in_ = interleave_views(name)
-            nc.scalar.copy(out=out[:, t0:t1], in_=in_[:, t0:t1])
+            nc.scalar.copy(out=out[:, :, :, t0:t1], in_=in_[:, :, :, t0:t1])
+
+        def il_gpsimd(name):
+            out, in_ = interleave_views(name)
+            nc.gpsimd.tensor_scalar(out=out, in0=in_, scalar1=1.0, scalar2=0.0, op0=MULT, op1=ADD)
 
         def il_cb():
-            out = cb_grp[:].rearrange("p (c j) -> p c j", j=PACK)
-            in_ = cb_raw[:].rearrange("p j c -> p c j")
+            out = cb_grp[:].rearrange("p (c i j) -> p c j i", i=4, j=PACK)
+            in_ = cb_raw[:].rearrange("p j (c i) -> p c j i", i=4)
             nc.vector.tensor_copy(out=out, in_=in_)
 
         def quant_cb():
@@ -148,42 +152,44 @@ def tile_learnedmodifiedgroupdelaycepstrum_x1_kernel(tc, x, wr, wi, vr, vi, g, c
 
         bank = {}
 
-        def mx1(kind, name, k):
+        def mx1(kind, name, k, cols=slice(0, 512)):
             acc = psum.tile([P, 4 * P], F32, name="bank")
-            cols = slice(P * (k % 4), P * (k % 4 + 1))
+            bank[(kind, k, cols.start)] = acc
+            rows = slice(P * (k % 4), P * (k % 4 + 1))
             w = weights[name]
             nc.tensor.matmul_mx(
-                out=acc[:],
-                lhsT=w["codes"][:, cols].bitcast(FP8X4),
-                lhsT_scale=w["scales"][:, cols],
-                rhs=x_codes[k // 4][:].bitcast(FP8X4),
-                rhs_scale=x_scales[k // 4][:],
+                out=acc[:, cols],
+                lhsT=w["codes"][:, rows].bitcast(FP8X4),
+                lhsT_scale=w["scales"][:, rows],
+                rhs=x_codes[k // 4][:, cols].bitcast(FP8X4),
+                rhs_scale=x_scales[k // 4][:, cols],
                 start=True,
                 stop=True,
             )
-            bank[(kind, k)] = acc
 
         sq = {}
 
-        def sq_scalar(kind, k):
-            s = flow.tile([P, F], F32, name="sq_" + kind)
-            nc.scalar.activation(out=s[:], in_=bank[(kind, k)][:], func=ACT.Square)
-            sq[(kind, k)] = s
+        def sq_scalar(kind, k, cols=slice(0, 512)):
+            if (kind, k) not in sq:
+                sq[(kind, k)] = flow.tile([P, F], F32, name="sq_" + kind)
+            nc.scalar.activation(out=sq[(kind, k)][:, cols], in_=bank[(kind, k, cols.start)][:, cols], func=ACT.Square)
 
-        def copy_x(kind, k, engine):
+        def copy_x(kind, k, engine, cols=slice(0, 512)):
             dst = xs_r[k] if kind == "r" else xs_i[k]
             if engine == "S":
-                nc.scalar.copy(out=dst[:], in_=bank[(kind, k)][:])
+                nc.scalar.copy(out=dst[:, cols], in_=bank[(kind, k, cols.start)][:, cols])
             else:
-                nc.vector.tensor_copy(out=dst[:], in_=bank[(kind, k)][:])
+                nc.vector.tensor_copy(out=dst[:, cols], in_=bank[(kind, k, cols.start)][:, cols])
 
         def p_add(k):
             eng = nc.vector if k in P_ADD_ON_VECTOR else nc.gpsimd
-            p_sum[k] = flow.tile([P, F], F32, name="p_sum")
-            eng.tensor_tensor(out=p_sum[k][:], in0=sq[("r", k)][:], in1=sq[("i", k)][:], op=ADD)
+            if k % 2 == 0:
+                p_sum[k // 2] = flow.tile([P, 2, F], F32, name="p_sum")
+            eng.tensor_tensor(out=p_sum[k // 2][:, k % 2, :], in0=sq[("r", k)][:], in1=sq[("i", k)][:], op=ADD)
 
         def ln(k):
-            nc.scalar.activation(out=lnp[k // 4][:, k % 4, :], in_=p_sum[k][:], func=ACT.Ln, bias=0.2)
+            t = k % 4
+            nc.scalar.activation(out=lnp[k // 4][:, t - 1 : t + 1, :], in_=p_sum[k // 2][:], func=ACT.Ln, bias=0.2)
 
         def exp(grp, n0, n1):
             nc.scalar.activation(out=ex[grp][:, :, n0:n1], in_=lnp[grp][:, :, n0:n1], func=ACT.Exp, scale=-0.7)
@@ -194,7 +200,7 @@ def tile_learnedmodifiedgroupdelaycepstrum_x1_kernel(tc, x, wr, wi, vr, vi, g, c
             t = k % 4
             nc.vector.scalar_tensor_tensor(
                 out=pr[(kind, k)][:],
-                in0=bank[("y" + kind, k)][:],
+                in0=bank[("y" + kind, k, 0)][:],
                 scalar=g_col[:, t : t + 1],
                 in1=src[k][:],
                 op0=MULT,
@@ -226,31 +232,34 @@ def tile_learnedmodifiedgroupdelaycepstrum_x1_kernel(tc, x, wr, wi, vr, vi, g, c
 
         def mx2(k):
             grp, s = k // 4, k % 4
-            for h in range(2):
-                if s == 0:
-                    out_bank[(grp, h)] = psum_tr.tile([P, 4, P], F32, name="tr") if grp == 0 else psum.tile([P, 4, P], F32, name="bank")
-                cols = slice(P * h, P * (h + 1))
-                rows = slice(P * s, P * (s + 1))
-                nc.tensor.matmul_mx(
-                    out=out_bank[(grp, h)][:, s, :],
-                    lhsT=tau_codes[grp][:, rows].bitcast(FP8X4),
-                    lhsT_scale=tau_scales[grp][:, rows],
-                    rhs=cb_codes[:, cols].bitcast(FP8X4),
-                    rhs_scale=cb_scales[:, cols],
-                    start=True,
-                    stop=True,
-                )
+            if k in (1, 3, 5):
+                bank2, slot = out_bank[k - 1], 1
+            else:
+                bank2, slot = (psum_tr.tile([P, 2, Q], F32, name="tr") if grp == 0 else psum.tile([P, 2, Q], F32, name="bank")), 0
+            out_bank[k] = bank2
+            rows = slice(P * s, P * (s + 1))
+            nc.tensor.matmul_mx(
+                out=bank2[:, slot, :],
+                lhsT=tau_codes[grp][:, rows].bitcast(FP8X4),
+                lhsT_scale=tau_scales[grp][:, rows],
+                rhs=cb_codes[:].bitcast(FP8X4),
+                rhs_scale=cb_scales[:],
+                start=True,
+                stop=True,
+            )
 
-        def out_32(grp, h, s0=0, s1=4):
-            nc.scalar.copy(out=o_32[grp][:, s0:s1, P * h : P * (h + 1)], in_=out_bank[(grp, h)][:, s0:s1, :])
-
-        def out_16(grp, h, engine):
-            dst = o_16[grp][:, 512 * h : 512 * (h + 1)].rearrange("p (q t) -> p q t", t=4)
-            src = out_bank[(grp, h)][:].rearrange("p t q -> p q t")
+        def out_32(k0, k1, engine):
+            dst = o_32[k0 // 4][:, k0 % 4 : k0 % 4 + k1 - k0, :]
+            src = out_bank[k0][:, 0 : k1 - k0, :]
             if engine == "S":
                 nc.scalar.copy(out=dst, in_=src)
             else:
                 nc.vector.tensor_copy(out=dst, in_=src)
+
+        def out_16(grp):
+            nc.vector.tensor_copy(
+                out=o_16[grp][:].rearrange("p (q t) -> p q t", t=4), in_=o_32[grp][:].rearrange("p t q -> p q t")
+            )
 
         def out_quant(grp):
             nc.vector.quantize_mx(out=o_codes[grp][:].bitcast(FP8X4), scales=o_scales[:, grp, :], in_=o_16[grp][:])
@@ -272,8 +281,8 @@ def tile_learnedmodifiedgroupdelaycepstrum_x1_kernel(tc, x, wr, wi, vr, vi, g, c
                 )
 
         load_x(0, 0, 2)
-        load_x(0, 2, 4)
         load_w("wr")
+        load_x(0, 2, 4)
         load_w("wi")
         load_x(1, 0, 4)
         load_w("vr")
@@ -284,56 +293,87 @@ def tile_learnedmodifiedgroupdelaycepstrum_x1_kernel(tc, x, wr, wi, vr, vi, g, c
         nc.vector.memset(warm[:], 1.0)
         nc.scalar.activation(out=warm[:], in_=warm[:], func=ACT.Ln)
         make_identity(nc, ident[:])
+        A = slice(0, 256)
+        B = slice(256, 512)
+
+        def use_x(kind, k, cols=slice(0, 512)):
+            eng = "S" if (kind, k) in COPY_ON_SCALAR else "V"
+            if (kind, k) in COPY_FIRST:
+                copy_x(kind, k, eng, cols)
+                sq_scalar(kind, k, cols)
+            else:
+                sq_scalar(kind, k, cols)
+                copy_x(kind, k, eng, cols)
 
         x_transpose(0, 0, 2)
         x_copy(0, 0, 2, "S")
-        x_transpose(0, 2, 4)
-        x_copy(0, 2, 4, cf("xe", "V"))
-        nc.gpsimd.tensor_copy(out=g_col[:], in_=g_raw[:])
-
-        def use_x(kind, k):
-            eng = "S" if (kind, k) in COPY_ON_SCALAR else "V"
-            if (kind, k) in COPY_FIRST:
-                copy_x(kind, k, eng)
-                sq_scalar(kind, k)
-            else:
-                sq_scalar(kind, k)
-                copy_x(kind, k, eng)
-
-        st = cf("wr_s", 3)
         il_vector("wr", 0, 2)
-        x_quant(0, 0, 2)
-        x_quant(0, 2, 4)
-        if st < 4:
-            il_scalar("wr", st, 4)
-        if st > 2:
-            il_vector("wr", 2, st)
         quant_w("wr", 0, 2)
-        mx1("r", "wr", 0)
-        mx1("r", "wr", 1)
-        quant_w("wr", 2, 4)
-        il_vector("wi", 0, cf("wi_s", 4))
-        if cf("wi_s", 4) < 4:
-            il_scalar("wi", cf("wi_s", 4), 4)
-        use_x("r", 0)
-        quant_w("wi", 0, 2)
-        quant_w("wi", 2, 4)
-        use_x("r", 1)
-        x_transpose(1, 0, 2)
-        x_transpose(1, 2, 4)
+        x_quant(0, 0, 2)
+        x_transpose(0, 2, 4)
+        if cf("o5", 0) == 0:
+            x_copy(0, 2, 4, "S")
+        mx1("r", "wr", 0, A)
+        mx1("r", "wr", 1, A)
+        use_x("r", 0, A)
+        if cf("o5", 0) == 1:
+            x_copy(0, 2, 4, "S")
+        use_x("r", 1, A)
+        if cf("o5", 0) == 2:
+            x_copy(0, 2, 4, "S")
+        if cf("o4", 0) == 0:
+            il_vector("wr", 2, 4)
+            x_quant(0, 2, 4)
+            il_vector("wi", 0, 2)
+            quant_w("wr", 2, 4)
+            quant_w("wi", 0, 2)
+            il_vector("wi", 2, 4)
+        if cf("o4", 0) == 1:
+            x_quant(0, 2, 4)
+            il_vector("wi", 0, 2)
+            il_vector("wr", 2, 4)
+            quant_w("wi", 0, 2)
+            il_vector("wi", 2, 4)
+            quant_w("wr", 2, 4)
+        if cf("o4", 0) == 2:
+            x_quant(0, 2, 4)
+            il_scalar("wr", 2, 4)
+            il_vector("wi", 0, 2)
+            quant_w("wr", 2, 4)
+            quant_w("wi", 0, 2)
+            il_vector("wi", 2, 4)
+        mx1("r", "wr", 0, B)
+        mx1("r", "wr", 1, B)
+        if cf("o6", 0) == 1:
+            x_transpose(1, 0, 2)
+            x_transpose(1, 2, 4)
+        use_x("r", 0, B)
         mx1("i", "wi", 0)
         mx1("i", "wi", 1)
-        x_copy(1, 0, 2, cf("xe0", "S"))
-        x_copy(1, 2, 4, cf("xe1", "S"))
+        if cf("o2", 0) == 0 and cf("o6", 0) == 0:
+            x_transpose(1, 0, 2)
+            x_transpose(1, 2, 4)
+        use_x("r", 1, B)
+        quant_w("wi", 2, 4)
+        if cf("o3", 0) == 0:
+            if cf("o2", 0) == 1 and cf("o6", 0) == 0:
+                x_transpose(1, 0, 2)
+                x_transpose(1, 2, 4)
+            x_copy(1, 0, 2, cf("xe0", "S"))
+            x_copy(1, 2, 4, cf("xe1", "S"))
 
         def early(step):
             if step == cf("e_qx1", 1):
                 x_quant(1, 0, 4)
-            if step == cf("e_ivr", 1):
+            if step == cf("e_ivr", 1) and not cf("vr_g", 1):
                 il_vector("vr", 0, 4)
+            if step == cf("g_ivr", 0) and cf("vr_g", 1):
+                il_gpsimd("vr")
+            if step == cf("g_ivi", 1) and cf("vi_g", 1):
+                il_gpsimd("vi")
             if step == cf("e_qvr", 1):
                 quant_w("vr")
-            if step == cf("e_ivi", 1):
+            if step == cf("e_ivi", 1) and not cf("vi_g", 1):
                 il_vector("vi", 0, 4)
             if step == cf("e_qvi", 1):
                 quant_w("vi")
@@ -341,82 +381,114 @@ def tile_learnedmodifiedgroupdelaycepstrum_x1_kernel(tc, x, wr, wi, vr, vi, g, c
                 il_cb()
             if step == cf("e_qcb", 1):
                 quant_cb()
+            if step == cf("g_g", 5):
+                nc.gpsimd.tensor_copy(out=g_col[:], in_=g_raw[:])
 
         def padds(step):
             for k in range(TILES):
                 if step == k + (cf("plv", 1) if k in P_ADD_ON_VECTOR else 0):
                     p_add(k)
-                if step == k + cf("lag", 2):
+                if step == k + cf("lag", 2) and k % 2 == 1:
                     ln(k)
 
         early(0)
         use_x("i", 0)
         padds(0)
         use_x("i", 1)
+        if cf("o3", 0) == 1:
+            if cf("o2", 0) == 1 and cf("o6", 0) == 0:
+                x_transpose(1, 0, 2)
+                x_transpose(1, 2, 4)
+            x_copy(1, 0, 2, cf("xe0", "S"))
+            x_copy(1, 2, 4, cf("xe1", "S"))
         early(1)
         padds(1)
-        for k in range(2, TILES):
-            mx1("r", "wr", k)
-            mx1("i", "wi", k)
-            use_x("r", k)
-            use_x("i", k)
-            early(k)
-            padds(k)
-        for k in range(TILES):
+        dy = cf("dy", 6)
+        f0 = cf("f0", 5)
+
+        def y_unit(k):
             mx1("yr", "vr", k)
             mx1("yi", "vi", k)
             prod("r", k)
             prod("i", k)
-            early(8 + k)
-            padds(8 + k)
-            if k == cf("lag", 2):
+            if k >= 1 + cf("nlag", 0):
+                n_add(k - 1 - cf("nlag", 0))
+            if f0 == k:
+                final(0, 0, 2)
+            if f0 + 1 == k:
+                final(0, 2, 4)
+            if f0 + cf("tq", 1) == k:
+                tau_quant(0, 0, 2)
+                mx2(0)
+                mx2(1)
+            if f0 + cf("tq", 1) + 1 == k:
+                tau_quant(0, 2, 4)
+                mx2(2)
+                mx2(3)
+
+        for k in range(2, TILES + dy):
+            if k < TILES:
+                mx1("r", "wr", k)
+                mx1("i", "wi", k)
+                if k == 2 and cf("o3", 0) == 2:
+                    if cf("o2", 0) == 1 and cf("o6", 0) == 0:
+                        x_transpose(1, 0, 2)
+                        x_transpose(1, 2, 4)
+                    x_copy(1, 0, 2, cf("xe0", "S"))
+                    x_copy(1, 2, 4, cf("xe1", "S"))
+                use_x("r", k)
+                if cf("yin", 0) and k >= dy:
+                    y_unit(k - dy)
+                use_x("i", k)
+            early(k)
+            padds(k)
+            if k == 7 + cf("lag", 2):
                 exp(0, 0, 256)
                 exp(0, 256, 512)
                 exp(1, 0, 256)
                 exp(1, 256, 512)
-            if k >= 1:
-                n_add(k - 1)
-            if cf("f0", 8) == k:
-                final(0, 0, 2)
-            if cf("f0", 8) + 1 == k:
-                final(0, 2, 4)
-        n_add(7)
-        if cf("f0", 8) > 7:
+            if k >= dy and not (cf("yin", 0) and k < TILES):
+                y_unit(k - dy)
+        if cf("nlag", 0):
+            n_add(6)
+        if cf("nl", 0) == 0:
+            n_add(7)
+        if f0 > 7:
             final(0, 0, 2)
-        if cf("f0", 8) > 6:
+        if f0 > 6:
             final(0, 2, 4)
-        tau_quant(0, 0, 2)
-        final(1, 0, 2)
-        tau_quant(0, 2, 4)
-        for k in range(4):
-            mx2(k)
-        out_16(0, 0, cf("oe0", "S"))
-        out_16(0, 1, cf("oe1", "S"))
-        out_32(0, 1)
-        out_32(0, 0)
+        if f0 + cf("tq", 1) > 7:
+            tau_quant(0, 0, 2)
+            mx2(0)
+            mx2(1)
+        if cf("nl", 0) == 1:
+            n_add(7)
+        if f0 + cf("tq", 1) > 6:
+            tau_quant(0, 2, 4)
+            mx2(2)
+            mx2(3)
+        out_32(0, 2, "S")
+        out_32(2, 4, "S")
         store_32(0)
+        final(1, 0, 2)
         final(1, 2, 3)
         tau_quant(1, 0, 2)
         mx2(4)
         mx2(5)
-        out_32(1, 0, 0, 2)
-        out_32(1, 1, 0, 2)
+        out_32(4, 6, "S")
         store_32(1, 0, 2)
         final(1, 3, 4)
-        if cf("oq", 1) == 0:
-            out_quant(0)
         tau_quant(1, 2, 3)
         mx2(6)
         tau_quant(1, 3, 4)
         mx2(7)
-        if cf("oq", 1) == 1:
-            out_quant(0)
+        out_16(0)
+        out_32(6, 7, "V")
+        out_quant(0)
         store_codes(0)
-        out_16(1, 1, "V")
-        out_16(1, 0, "S")
-        out_32(1, 1, 2, 4)
-        out_32(1, 0, 2, 4)
-        out_quant(1)
+        out_32(7, 8, "S")
         store_32(1, 2, 4)
+        out_16(1)
+        out_quant(1)
         store_codes(1)
         store_scales()

from contextlib import ExitStack

import concourse.mybir as mybir
from concourse.masks import make_identity

F32 = mybir.dt.float32
BF16 = mybir.dt.bfloat16
I32 = mybir.dt.int32
U32 = mybir.dt.uint32
U8 = mybir.dt.uint8
FP8X4 = mybir.dt.float8_e4m3fn_x4
ADD = mybir.AluOpType.add
MULT = mybir.AluOpType.mult
ACT = mybir.ActivationFunctionType

P = 128
PACK = 4
N, L, F, Q = 1024, 512, 512, 256
GROUPS = 2
TILES = 8
FLOPS = 2 * N * L * F * 4 + 2 * N * F * Q

CFG = {"xe0": "S", "e_qvr": 2, "nv": (6, 7), "o5": 0, "e_ivr": 0, "cs": (("i", 0), ("i", 1), ("i", 2), ("i", 3), ("i", 4), ("i", 6), ("i", 7), ("r", 0), ("r", 1), ("r", 5), ("r", 7)), "tq": 2, "pv": (0, 2, 3, 6), "vr_g": 0, "o3": 2, "g_g": 2, "e_ivi": 1, "f0": 8, "vf": (("i", 0), ("i", 3), ("i", 6), ("r", 1), ("r", 5)), "xe1": "S", "nacc": 6, "g_ivr": 1, "e32": 1, "fb": 4, "e_qvi": 3, "e_qcb": 6, "e_icb": 4, "o2": 0, "plv": 0, "tl": 3, "lag": 3, "vi_g": 0, "g_ivi": 5, "nl": 0, "o4": 0, "e_qx1": 2, "nlag": 0, "yin": 1, "dy": 4, "oo": 1, "o6": 0}


def cf(k, d):
    return CFG.get(k, d)
COPY_ON_SCALAR = cf("cs", (("r", 0), ("i", 0), ("r", 1), ("i", 1), ("r", 2), ("i", 2)))
COPY_FIRST = cf("vf", ())
P_ADD_ON_VECTOR = cf("pv", (0, 1))
NADD_ON_VECTOR = cf("nv", (7,))
NACC = cf("nacc", 6)


def tile_learnedmodifiedgroupdelaycepstrum_x1_kernel(tc, x, wr, wi, vr, vi, g, cb, out_0, out_1, out_2):
    nc = tc.nc
    with ExitStack() as ctx:
        keep = ctx.enter_context(tc.tile_pool(name="keep", bufs=1))
        flow = ctx.enter_context(tc.tile_pool(name="flow", bufs=cf("fb", 4)))
        psum = ctx.enter_context(tc.psum_pool(name="psum", bufs=NACC))
        psum_tr = ctx.enter_context(tc.psum_pool(name="psum_tr", bufs=8 - NACC))
        ctx.enter_context(tc.manual_schedule())

        weights = {}
        for name, src in (("wr", wr), ("wi", wi), ("vr", vr), ("vi", vi)):
            weights[name] = dict(
                src=src,
                raw=keep.tile([P, PACK, F], BF16, name="raw_" + name, align_bytes=64),
                grp=keep.tile([P, F * PACK], BF16, name="grp_" + name, align_bytes=64),
                codes=keep.tile([P, F], U32, name="codes_" + name, align_bytes=64),
                scales=keep.tile([P, F], U8, name="scales_" + name, align_bytes=64),
            )
        cb_raw = keep.tile([P, PACK, Q], BF16, name="cb_raw", align_bytes=64)
        cb_grp = keep.tile([P, Q * PACK], BF16, name="cb_grp", align_bytes=64)
        cb_codes = keep.tile([P, Q], U32, name="cb_codes", align_bytes=64)
        cb_scales = keep.tile([P, Q], U8, name="cb_scales", align_bytes=64)
        g_raw = keep.tile([P, PACK], BF16, name="g_raw")
        g_col = keep.tile([P, PACK], F32, name="g_col")
        x_raw = [keep.tile([P, 4, L], BF16, name=f"x_raw{i}", align_bytes=64) for i in range(GROUPS)]
        x_grp = [keep.tile([P, 4 * P * PACK], BF16, name=f"x_grp{i}", align_bytes=64) for i in range(GROUPS)]
        x_codes = [keep.tile([P, 4 * P], U32, name=f"x_codes{i}", align_bytes=64) for i in range(GROUPS)]
        x_scales = [keep.tile([P, 4 * P], U8, name=f"x_scales{i}", align_bytes=64) for i in range(GROUPS)]
        xs_r = [keep.tile([P, F], F32, name=f"xs_r{i}") for i in range(TILES)]
        xs_i = [keep.tile([P, F], F32, name=f"xs_i{i}") for i in range(TILES)]
        p_sum = {}
        pr = {}
        lnp = [keep.tile([P, PACK, 4 * P], F32, name=f"lnp{i}") for i in range(GROUPS)]
        ex = [keep.tile([P, PACK, 4 * P], F32, name=f"ex{i}") for i in range(GROUPS)]
        num = [keep.tile([P, PACK, 4 * P], F32, name=f"num{i}") for i in range(GROUPS)]
        tau = [keep.tile([P, 4 * P * PACK], BF16, name=f"tau{i}", align_bytes=64) for i in range(GROUPS)]
        tau_codes = [keep.tile([P, 4 * P], U32, name=f"tau_codes{i}", align_bytes=64) for i in range(GROUPS)]
        tau_scales = [keep.tile([P, 4 * P], U8, name=f"tau_scales{i}", align_bytes=64) for i in range(GROUPS)]
        o_32 = [keep.tile([P, 4, Q], F32, name=f"o_32_{i}", align_bytes=64) for i in range(GROUPS)]
        o_16 = [keep.tile([P, Q * PACK], BF16, name=f"o_16_{i}", align_bytes=64) for i in range(GROUPS)]
        o_codes = [keep.tile([P, Q], U32, name=f"o_codes{i}", align_bytes=64) for i in range(GROUPS)]
        o_scales = keep.tile([P, GROUPS, Q], U8, name="o_scales", align_bytes=64)
        ident = keep.tile([P, P], F32, name="ident")
        warm = keep.tile([P, 1], F32, name="warm")

        def load_w(name):
            w = weights[name]
            nc.sync.dma_start(out=w["raw"][:], in_=w["src"].rearrange("(p j) c -> p j c", j=PACK))

        def load_x(grp, t0, t1):
            src = x[512 * grp : 512 * (grp + 1), :].rearrange("(p t) k -> p t k", t=4)
            nc.sync.dma_start(out=x_raw[grp][:, t0:t1, :], in_=src[:, t0:t1, :])

        def interleave_views(name):
            w = weights[name]
            out = w["grp"][:].rearrange("p (t m j) -> p m j t", t=4, j=PACK)
            in_ = w["raw"][:].rearrange("p j (m t) -> p m j t", t=4)
            return out, in_

        def il_vector(name, t0, t1):
            out, in_ = interleave_views(name)
            nc.vector.tensor_copy(out=out[:, :, :, t0:t1], in_=in_[:, :, :, t0:t1])

        def il_scalar(name, t0, t1):
            out, in_ = interleave_views(name)
            nc.scalar.copy(out=out[:, :, :, t0:t1], in_=in_[:, :, :, t0:t1])

        def il_gpsimd(name):
            out, in_ = interleave_views(name)
            nc.gpsimd.tensor_scalar(out=out, in0=in_, scalar1=1.0, scalar2=0.0, op0=MULT, op1=ADD)

        def il_cb():
            out = cb_grp[:].rearrange("p (c i j) -> p c j i", i=4, j=PACK)
            in_ = cb_raw[:].rearrange("p j (c i) -> p c j i", i=4)
            nc.vector.tensor_copy(out=out, in_=in_)

        def quant_cb():
            nc.vector.quantize_mx(out=cb_codes[:].bitcast(FP8X4), scales=cb_scales[:], in_=cb_grp[:])

        def quant_w(name, t0=0, t1=4):
            w = weights[name]
            cols = slice(P * t0, P * t1)
            nc.vector.quantize_mx(
                out=w["codes"][:, cols].bitcast(FP8X4),
                scales=w["scales"][:, cols],
                in_=w["grp"][:, PACK * P * t0 : PACK * P * t1],
            )


        x_bank = {}

        def x_transpose(grp, s0, s1):
            words = x_raw[grp][:].rearrange("p t k -> p (t k)").bitcast(F32)
            for s in range(s0, s1):
                if s % 2 == 0:
                    x_bank[(grp, s // 2)] = psum_tr.tile([P, 2, 2, P], F32, name="tr")
                base = s * (L // 2)
                for u in range(2):
                    nc.tensor.transpose(
                        x_bank[(grp, s // 2)][:, s % 2, u, :], words[:, base + u : base + L // 2 : 2], ident[:]
                    )

        def x_copy(grp, s0, s1, engine):
            out = x_grp[grp][:, 512 * s0 : 512 * s1].bitcast(F32).rearrange("p (t r u) -> p t r u", t=s1 - s0, u=2)
            src = x_bank[(grp, s0 // 2)][:, s0 % 2 : s0 % 2 + s1 - s0].rearrange("p t u r -> p t r u")
            if engine == "S":
                nc.scalar.copy(out=out, in_=src)
            else:
                nc.vector.tensor_copy(out=out, in_=src)

        def x_quant(grp, s0, s1):
            cols = slice(P * s0, P * s1)
            nc.vector.quantize_mx(
                out=x_codes[grp][:, cols].bitcast(FP8X4),
                scales=x_scales[grp][:, cols],
                in_=x_grp[grp][:, 512 * s0 : 512 * s1],
            )

        bank = {}

        def mx1(kind, name, k, cols=slice(0, 512)):
            acc = psum.tile([P, 4 * P], F32, name="bank")
            bank[(kind, k, cols.start)] = acc
            rows = slice(P * (k % 4), P * (k % 4 + 1))
            w = weights[name]
            nc.tensor.matmul_mx(
                out=acc[:, cols],
                lhsT=w["codes"][:, rows].bitcast(FP8X4),
                lhsT_scale=w["scales"][:, rows],
                rhs=x_codes[k // 4][:, cols].bitcast(FP8X4),
                rhs_scale=x_scales[k // 4][:, cols],
                start=True,
                stop=True,
            )

        sq = {}

        def sq_scalar(kind, k, cols=slice(0, 512)):
            if (kind, k) not in sq:
                sq[(kind, k)] = flow.tile([P, F], F32, name="sq_" + kind)
            nc.scalar.activation(out=sq[(kind, k)][:, cols], in_=bank[(kind, k, cols.start)][:, cols], func=ACT.Square)

        def copy_x(kind, k, engine, cols=slice(0, 512)):
            dst = xs_r[k] if kind == "r" else xs_i[k]
            if engine == "S":
                nc.scalar.copy(out=dst[:, cols], in_=bank[(kind, k, cols.start)][:, cols])
            else:
                nc.vector.tensor_copy(out=dst[:, cols], in_=bank[(kind, k, cols.start)][:, cols])

        def p_add(k):
            eng = nc.vector if k in P_ADD_ON_VECTOR else nc.gpsimd
            if k % 2 == 0:
                p_sum[k // 2] = flow.tile([P, 2, F], F32, name="p_sum")
            eng.tensor_tensor(out=p_sum[k // 2][:, k % 2, :], in0=sq[("r", k)][:], in1=sq[("i", k)][:], op=ADD)

        def ln(k):
            t = k % 4
            nc.scalar.activation(out=lnp[k // 4][:, t - 1 : t + 1, :], in_=p_sum[k // 2][:], func=ACT.Ln, bias=0.2)

        def exp(grp, n0, n1):
            nc.scalar.activation(out=ex[grp][:, :, n0:n1], in_=lnp[grp][:, :, n0:n1], func=ACT.Exp, scale=-0.7)

        def prod(kind, k):
            src = xs_r if kind == "r" else xs_i
            pr[(kind, k)] = flow.tile([P, F], F32, name="pr_" + kind)
            t = k % 4
            nc.vector.scalar_tensor_tensor(
                out=pr[(kind, k)][:],
                in0=bank[("y" + kind, k, 0)][:],
                scalar=g_col[:, t : t + 1],
                in1=src[k][:],
                op0=MULT,
                op1=MULT,
            )

        def n_add(k):
            eng = nc.vector if k in NADD_ON_VECTOR else nc.gpsimd
            eng.tensor_tensor(out=num[k // 4][:, k % 4, :], in0=pr[("r", k)][:], in1=pr[("i", k)][:], op=ADD)

        def final(grp, s0, s1):
            toks = slice(P * s0, P * s1)
            nc.vector.tensor_tensor(
                out=tau[grp][:, 512 * s0 : 512 * s1].rearrange("p (c i t) -> p c t i", i=4, t=PACK),
                in0=num[grp][:, :, toks].rearrange("p t (c i) -> p c t i", i=4),
                in1=ex[grp][:, :, toks].rearrange("p t (c i) -> p c t i", i=4),
                op=MULT,
            )

        def tau_quant(grp, s0, s1):
            cols = slice(P * s0, P * s1)
            nc.vector.quantize_mx(
                out=tau_codes[grp][:, cols].bitcast(FP8X4),
                scales=tau_scales[grp][:, cols],
                in_=tau[grp][:, 512 * s0 : 512 * s1],
            )

        out_bank = {}

        def mx2(k):
            grp, s = k // 4, k % 4
            if k in (1, 3, 5):
                bank2, slot = out_bank[k - 1], 1
            else:
                bank2, slot = (psum_tr.tile([P, 2, Q], F32, name="tr") if grp == 0 else psum.tile([P, 2, Q], F32, name="bank")), 0
            out_bank[k] = bank2
            rows = slice(P * s, P * (s + 1))
            nc.tensor.matmul_mx(
                out=bank2[:, slot, :],
                lhsT=tau_codes[grp][:, rows].bitcast(FP8X4),
                lhsT_scale=tau_scales[grp][:, rows],
                rhs=cb_codes[:].bitcast(FP8X4),
                rhs_scale=cb_scales[:],
                start=True,
                stop=True,
            )

        def out_32(k0, k1, engine):
            dst = o_32[k0 // 4][:, k0 % 4 : k0 % 4 + k1 - k0, :]
            src = out_bank[k0][:, 0 : k1 - k0, :]
            if engine == "S":
                nc.scalar.copy(out=dst, in_=src)
            else:
                nc.vector.tensor_copy(out=dst, in_=src)

        def out_16(grp):
            nc.vector.tensor_copy(
                out=o_16[grp][:].rearrange("p (q t) -> p q t", t=4), in_=o_32[grp][:].rearrange("p t q -> p q t")
            )

        def out_quant(grp):
            nc.vector.quantize_mx(out=o_codes[grp][:].bitcast(FP8X4), scales=o_scales[:, grp, :], in_=o_16[grp][:])

        def store_32(grp, s0=0, s1=4):
            dst = out_0[512 * grp : 512 * (grp + 1), :].rearrange("(p t) m -> p t m", t=4)
            nc.sync.dma_start(out=dst[:, s0:s1, :], in_=o_32[grp][:, s0:s1, :])

        def store_codes(grp):
            nc.sync.dma_start(
                out=out_1[grp].rearrange("p m t -> p (m t)").bitcast(I32), in_=o_codes[grp][:].bitcast(I32)
            )

        def store_scales():
            for quad in range(4):
                nc.sync.dma_start(
                    out=out_2[:, 4 * quad : 4 * quad + 4, :].bitcast(I32).rearrange("g q m -> q g m"),
                    in_=o_scales[32 * quad : 32 * quad + 4, :, :].bitcast(I32),
                )

        load_x(0, 0, 2)
        load_w("wr")
        load_x(0, 2, 4)
        load_w("wi")
        load_x(1, 0, 4)
        load_w("vr")
        load_w("vi")
        nc.sync.dma_start(out=cb_raw[:], in_=cb.rearrange("(p j) c -> p j c", j=PACK))
        nc.sync.dma_start(out=g_raw[:], in_=g.rearrange("(p t) -> p t", t=PACK))

        nc.vector.memset(warm[:], 1.0)
        nc.scalar.activation(out=warm[:], in_=warm[:], func=ACT.Ln)
        make_identity(nc, ident[:])
        A = slice(0, 256)
        B = slice(256, 512)

        def use_x(kind, k, cols=slice(0, 512)):
            eng = "S" if (kind, k) in COPY_ON_SCALAR else "V"
            if (kind, k) in COPY_FIRST:
                copy_x(kind, k, eng, cols)
                sq_scalar(kind, k, cols)
            else:
                sq_scalar(kind, k, cols)
                copy_x(kind, k, eng, cols)

        x_transpose(0, 0, 2)
        x_copy(0, 0, 2, "S")
        il_vector("wr", 0, 2)
        quant_w("wr", 0, 2)
        x_quant(0, 0, 2)
        x_transpose(0, 2, 4)
        if cf("o5", 0) == 0:
            x_copy(0, 2, 4, "S")
        mx1("r", "wr", 0, A)
        mx1("r", "wr", 1, A)
        use_x("r", 0, A)
        if cf("o5", 0) == 1:
            x_copy(0, 2, 4, "S")
        use_x("r", 1, A)
        if cf("o5", 0) == 2:
            x_copy(0, 2, 4, "S")
        if cf("o4", 0) == 0:
            il_vector("wr", 2, 4)
            x_quant(0, 2, 4)
            il_vector("wi", 0, 2)
            quant_w("wr", 2, 4)
            quant_w("wi", 0, 2)
            il_vector("wi", 2, 4)
        if cf("o4", 0) == 1:
            x_quant(0, 2, 4)
            il_vector("wi", 0, 2)
            il_vector("wr", 2, 4)
            quant_w("wi", 0, 2)
            il_vector("wi", 2, 4)
            quant_w("wr", 2, 4)
        if cf("o4", 0) == 2:
            x_quant(0, 2, 4)
            il_scalar("wr", 2, 4)
            il_vector("wi", 0, 2)
            quant_w("wr", 2, 4)
            quant_w("wi", 0, 2)
            il_vector("wi", 2, 4)
        mx1("r", "wr", 0, B)
        mx1("r", "wr", 1, B)
        if cf("o6", 0) == 1:
            x_transpose(1, 0, 2)
            x_transpose(1, 2, 4)
        use_x("r", 0, B)
        mx1("i", "wi", 0)
        mx1("i", "wi", 1)
        if cf("o2", 0) == 0 and cf("o6", 0) == 0:
            x_transpose(1, 0, 2)
            x_transpose(1, 2, 4)
        use_x("r", 1, B)
        quant_w("wi", 2, 4)
        if cf("o3", 0) == 0:
            if cf("o2", 0) == 1 and cf("o6", 0) == 0:
                x_transpose(1, 0, 2)
                x_transpose(1, 2, 4)
            x_copy(1, 0, 2, cf("xe0", "S"))
            x_copy(1, 2, 4, cf("xe1", "S"))

        def early(step):
            if step == cf("e_qx1", 1):
                x_quant(1, 0, 4)
            if step == cf("e_ivr", 1) and not cf("vr_g", 1):
                il_vector("vr", 0, 4)
            if step == cf("g_ivr", 0) and cf("vr_g", 1):
                il_gpsimd("vr")
            if step == cf("g_ivi", 1) and cf("vi_g", 1):
                il_gpsimd("vi")
            if step == cf("e_qvr", 1):
                quant_w("vr")
            if step == cf("e_ivi", 1) and not cf("vi_g", 1):
                il_vector("vi", 0, 4)
            if step == cf("e_qvi", 1):
                quant_w("vi")
            if step == cf("e_icb", 1):
                il_cb()
            if step == cf("e_qcb", 1):
                quant_cb()
            if step == cf("g_g", 5):
                nc.gpsimd.tensor_copy(out=g_col[:], in_=g_raw[:])

        def padds(step):
            for k in range(TILES):
                if step == k + (cf("plv", 1) if k in P_ADD_ON_VECTOR else 0):
                    p_add(k)
                if step == k + cf("lag", 2) and k % 2 == 1:
                    ln(k)

        early(0)
        use_x("i", 0)
        padds(0)
        use_x("i", 1)
        if cf("o3", 0) == 1:
            if cf("o2", 0) == 1 and cf("o6", 0) == 0:
                x_transpose(1, 0, 2)
                x_transpose(1, 2, 4)
            x_copy(1, 0, 2, cf("xe0", "S"))
            x_copy(1, 2, 4, cf("xe1", "S"))
        early(1)
        padds(1)
        dy = cf("dy", 6)
        f0 = cf("f0", 5)

        def y_unit(k):
            mx1("yr", "vr", k)
            mx1("yi", "vi", k)
            prod("r", k)
            prod("i", k)
            if k >= 1 + cf("nlag", 0):
                n_add(k - 1 - cf("nlag", 0))
            if f0 == k:
                final(0, 0, 2)
            if f0 + 1 == k:
                final(0, 2, 4)
            if f0 + cf("tq", 1) == k:
                tau_quant(0, 0, 2)
                mx2(0)
                mx2(1)
            if f0 + cf("tq", 1) + 1 == k:
                tau_quant(0, 2, 4)
                mx2(2)
                mx2(3)

        for k in range(2, TILES + dy):
            if k < TILES:
                mx1("r", "wr", k)
                mx1("i", "wi", k)
                if k == 2 and cf("o3", 0) == 2:
                    if cf("o2", 0) == 1 and cf("o6", 0) == 0:
                        x_transpose(1, 0, 2)
                        x_transpose(1, 2, 4)
                    x_copy(1, 0, 2, cf("xe0", "S"))
                    x_copy(1, 2, 4, cf("xe1", "S"))
                use_x("r", k)
                if cf("yin", 0) and k >= dy:
                    y_unit(k - dy)
                use_x("i", k)
            early(k)
            padds(k)
            if k == 7 + cf("lag", 2):
                exp(0, 0, 256)
                exp(0, 256, 512)
                exp(1, 0, 256)
                exp(1, 256, 512)
            if k >= dy and not (cf("yin", 0) and k < TILES):
                y_unit(k - dy)
        if cf("nlag", 0):
            n_add(6)
        if cf("nl", 0) == 0:
            n_add(7)
        if f0 > 7:
            final(0, 0, 2)
        if f0 > 6:
            final(0, 2, 4)
        if f0 + cf("tq", 1) > 7:
            tau_quant(0, 0, 2)
            mx2(0)
            mx2(1)
        if cf("nl", 0) == 1:
            n_add(7)
        if f0 + cf("tq", 1) > 6:
            tau_quant(0, 2, 4)
            mx2(2)
            mx2(3)
        out_32(0, 2, "S")
        out_32(2, 4, "S")
        store_32(0)
        final(1, 0, 2)
        final(1, 2, 3)
        tau_quant(1, 0, 2)
        mx2(4)
        mx2(5)
        out_32(4, 6, "S")
        store_32(1, 0, 2)
        final(1, 3, 4)
        tau_quant(1, 2, 3)
        mx2(6)
        tau_quant(1, 3, 4)
        mx2(7)
        out_16(0)
        out_32(6, 7, "V")
        out_quant(0)
        store_codes(0)
        out_32(7, 8, "S")
        store_32(1, 2, 4)
        out_16(1)
        out_quant(1)
        store_codes(1)
        store_scales()
